import numpy as np
import ml_dtypes

BF16 = ml_dtypes.bfloat16


def bf(x):
    return np.asarray(x, np.float32).astype(BF16)


def f32(x):
    return np.asarray(x, np.float32)


def f64(x):
    return np.asarray(x).astype(np.float64)


def striped(idx):
    return np.tile(idx.reshape(-1, 16).T, (8, 1))


S, K, M, N, E, Q = 512, 512, 128, 384, 4, 96


def setup_inputs():
    return {"base": bf(np.random.standard_normal((M, S))), "x": bf(np.random.standard_normal((K, N))), "w": bf(np.random.standard_normal((E, K, M)) / np.sqrt(K)), "s": f32(0.5 + np.random.random_sample((M, 1))), "b": f32(0.5 * np.random.standard_normal((M, 1))), "offs": striped(np.random.permutation(S)[:N])}


def reference(base, x, w, s, b, offs):
    idx = offs[:16].T.reshape(-1)
    z = f64(base).copy()
    for e in range(E):
        z[:, idx[e * Q : (e + 1) * Q]] += f64(w)[e].T @ f64(x)[:, e * Q : (e + 1) * Q]
    return z * f64(s) + f64(b)

@@ -1,0 +1,61 @@
+import concourse.mybir as mybir
+from concourse.masks import make_identity
+
+BF16, F32, U16 = mybir.dt.bfloat16, mybir.dt.float32, mybir.dt.uint16
+MULT, ADD = mybir.AluOpType.mult, mybir.AluOpType.add
+
+P = 128
+S = 512
+K = 512
+N = 384
+E = 4
+Q = N // E
+KB = K // P
+QC = Q // 16
+
+FLOPS = 2 * K * P * N
+
+
+def tile_scatter_matmul_kernel(tc, base, x, w, s, b, offs, out):
+    nc = tc.nc
+    with (
+        tc.tile_pool(name="held", bufs=1) as held,
+        tc.psum_pool(name="psum", bufs=1) as psum,
+    ):
+        offsets = held.tile([P, N // 16], U16, name="offsets")
+        nc.sync.dma_start(offsets[:], offs)
+
+        base_sb = held.tile([P, S], BF16, name="base_sb")
+        nc.scalar.dma_start(base_sb[:], base)
+
+        x_sb = held.tile([P, KB, N], BF16, name="x_sb")
+        nc.sync.dma_start(x_sb[:], x.rearrange("(kb p) n -> p kb n", p=P))
+
+        w_sb = held.tile([P, E * KB, P], BF16, name="w_sb")
+        nc.scalar.dma_start(w_sb[:], w.rearrange("e (kb p) m -> p (e kb) m", p=P))
+
+        gain = held.tile([P, 1], F32, name="gain")
+        nc.gpsimd.dma_start(gain[:], s)
+        shift = held.tile([P, 1], F32, name="shift")
+        nc.gpsimd.dma_start(shift[:], b)
+
+        ident = held.tile([P, P], BF16, name="ident")
+        make_identity(nc, ident[:])
+
+        window = psum.tile([P, S], F32, name="window")
+        nc.tensor.matmul(window[:], ident[:], base_sb[:], start=True, stop=False)
+
+        for e in range(E):
+            piece = offsets[:, e * QC : (e + 1) * QC]
+            for kb in range(KB):
+                nc.tensor.matmul(
+                    window[:].indirect(piece),
+                    w_sb[:, e * KB + kb, :],
+                    x_sb[:, kb, e * Q : (e + 1) * Q],
+                    start=False,
+                    stop=(e == E - 1 and kb == KB - 1),
+                )
+
+        result = held.tile([P, S], F32, name="result")
+        nc.vector.tensor_scalar(result[:], window[:], gain[:], shift[:], MULT, ADD)
+        nc.sync.dma_start(out, result[:])

@@ -25,22 +25,26 @@ def tile_scatter_matmul_kernel(tc, base, x, w, s, b, offs, out):
         offsets = held.tile([P, N // 16], U16, name="offsets")
         nc.sync.dma_start(offsets[:], offs)
 
+        ident = held.tile([P, P], BF16, name="ident")
+        make_identity(nc, ident[:])
+
         base_sb = held.tile([P, S], BF16, name="base_sb")
         nc.scalar.dma_start(base_sb[:], base)
 
         x_sb = held.tile([P, KB, N], BF16, name="x_sb")
-        nc.sync.dma_start(x_sb[:], x.rearrange("(kb p) n -> p kb n", p=P))
+        nc.sync.dma_start(x_sb[:], x.rearrange("(p kb) n -> p kb n", kb=KB))
 
-        w_sb = held.tile([P, E * KB, P], BF16, name="w_sb")
-        nc.scalar.dma_start(w_sb[:], w.rearrange("e (kb p) m -> p (e kb) m", p=P))
+        w_sb = []
+        for e in range(E):
+            w_e = held.tile([P, KB, P], BF16, name=f"w{e}")
+            queue = nc.scalar if e % 2 == 0 else nc.sync
+            queue.dma_start(w_e[:], w[e].rearrange("(p kb) m -> p kb m", kb=KB))
+            w_sb.append(w_e)
 
         gain = held.tile([P, 1], F32, name="gain")
-        nc.gpsimd.dma_start(gain[:], s)
+        nc.scalar.dma_start(gain[:], s)
         shift = held.tile([P, 1], F32, name="shift")
-        nc.gpsimd.dma_start(shift[:], b)
-
-        ident = held.tile([P, P], BF16, name="ident")
-        make_identity(nc, ident[:])
+        nc.sync.dma_start(shift[:], b)
 
         window = psum.tile([P, S], F32, name="window")
         nc.tensor.matmul(window[:], ident[:], base_sb[:], start=True, stop=False)
@@ -50,7 +54,7 @@ def tile_scatter_matmul_kernel(tc, base, x, w, s, b, offs, out):
             for kb in range(KB):
                 nc.tensor.matmul(
                     window[:].indirect(piece),
-                    w_sb[:, e * KB + kb, :],
+                    w_sb[e][:, kb, :],
                     x_sb[:, kb, e * Q : (e + 1) * Q],
                     start=False,
                     stop=(e == E - 1 and kb == KB - 1),

@@ -11,6 +11,7 @@ N = 384
 E = 4
 Q = N // E
 KB = K // P
+HB = KB // 2
 QC = Q // 16
 
 FLOPS = 2 * K * P * N
@@ -31,15 +32,18 @@ def tile_scatter_matmul_kernel(tc, base, x, w, s, b, offs, out):
         base_sb = held.tile([P, S], BF16, name="base_sb")
         nc.scalar.dma_start(base_sb[:], base)
 
-        x_sb = held.tile([P, KB, N], BF16, name="x_sb")
-        nc.sync.dma_start(x_sb[:], x.rearrange("(p kb) n -> p kb n", kb=KB))
-
-        w_sb = []
-        for e in range(E):
-            w_e = held.tile([P, KB, P], BF16, name=f"w{e}")
-            queue = nc.scalar if e % 2 == 0 else nc.sync
-            queue.dma_start(w_e[:], w[e].rearrange("(p kb) m -> p kb m", kb=KB))
-            w_sb.append(w_e)
+        x_view = x.rearrange("(p kb) n -> p kb n", kb=KB)
+        x_sb, w_sb = [], []
+        for h in range(2):
+            blocks = slice(h * HB, (h + 1) * HB)
+            x_h = held.tile([P, HB, N], BF16, name=f"x{h}")
+            (nc.sync if h == 0 else nc.scalar).dma_start(x_h[:], x_view[:, blocks, :])
+            x_sb.append(x_h)
+            for e in range(E):
+                w_he = held.tile([P, HB, P], BF16, name=f"w{h}_{e}")
+                queue = nc.scalar if e % 2 == 0 else nc.sync
+                queue.dma_start(w_he[:], w[e].rearrange("(p kb) m -> p kb m", kb=KB)[:, blocks, :])
+                w_sb.append(w_he)
 
         gain = held.tile([P, 1], F32, name="gain")
         nc.scalar.dma_start(gain[:], s)
@@ -49,16 +53,17 @@ def tile_scatter_matmul_kernel(tc, base, x, w, s, b, offs, out):
         window = psum.tile([P, S], F32, name="window")
         nc.tensor.matmul(window[:], ident[:], base_sb[:], start=True, stop=False)
 
-        for e in range(E):
-            piece = offsets[:, e * QC : (e + 1) * QC]
-            for kb in range(KB):
-                nc.tensor.matmul(
-                    window[:].indirect(piece),
-                    w_sb[e][:, kb, :],
-                    x_sb[:, kb, e * Q : (e + 1) * Q],
-                    start=False,
-                    stop=(e == E - 1 and kb == KB - 1),
-                )
+        for h in range(2):
+            for e in range(E):
+                piece = offsets[:, e * QC : (e + 1) * QC]
+                for q in range(HB):
+                    nc.tensor.matmul(
+                        window[:].indirect(piece),
+                        w_sb[h * E + e][:, q, :],
+                        x_sb[h][:, q, e * Q : (e + 1) * Q],
+                        start=False,
+                        stop=(h == 1 and e == E - 1 and q == HB - 1),
+                    )
 
         result = held.tile([P, S], F32, name="result")
         nc.vector.tensor_scalar(result[:], window[:], gain[:], shift[:], MULT, ADD)

@@ -12,6 +12,7 @@ E = 4
 Q = N // E
 KB = K // P
 HB = KB // 2
+WARM = 4
 QC = Q // 16
 
 FLOPS = 2 * K * P * N
@@ -25,6 +26,12 @@ def tile_scatter_matmul_kernel(tc, base, x, w, s, b, offs, out):
     ):
         offsets = held.tile([P, N // 16], U16, name="offsets")
         nc.sync.dma_start(offsets[:], offs)
+
+        zeros = held.tile([P, S], BF16, name="zeros")
+        nc.vector.memset(zeros[:], 0.0)
+        spare = psum.tile([P, S], F32, name="spare")
+        for i in range(WARM):
+            nc.tensor.matmul(spare[:], zeros[:, 0:P], zeros[:], start=True, stop=True)
 
         ident = held.tile([P, P], BF16, name="ident")
         make_identity(nc, ident[:])

@@ -12,7 +12,7 @@ E = 4
 Q = N // E
 KB = K // P
 HB = KB // 2
-WARM = 4
+WARM = 8
 QC = Q // 16
 
 FLOPS = 2 * K * P * N
@@ -27,11 +27,11 @@ def tile_scatter_matmul_kernel(tc, base, x, w, s, b, offs, out):
         offsets = held.tile([P, N // 16], U16, name="offsets")
         nc.sync.dma_start(offsets[:], offs)
 
-        zeros = held.tile([P, S], BF16, name="zeros")
+        zeros = held.tile([P, P], BF16, name="zeros")
         nc.vector.memset(zeros[:], 0.0)
-        spare = psum.tile([P, S], F32, name="spare")
+        spare = psum.tile([P, P], F32, name="spare")
         for i in range(WARM):
-            nc.tensor.matmul(spare[:], zeros[:, 0:P], zeros[:], start=True, stop=True)
+            nc.tensor.matmul(spare[:], zeros[:], zeros[:], start=True, stop=True)
 
         ident = held.tile([P, P], BF16, name="ident")
         make_identity(nc, ident[:])
@@ -73,5 +73,7 @@ def tile_scatter_matmul_kernel(tc, base, x, w, s, b, offs, out):
                     )
 
         result = held.tile([P, S], F32, name="result")
-        nc.vector.tensor_scalar(result[:], window[:], gain[:], shift[:], MULT, ADD)
-        nc.sync.dma_start(out, result[:])
+        for half, queue in enumerate((nc.sync, nc.scalar)):
+            cols = slice(half * (S // 2), (half + 1) * (S // 2))
+            nc.vector.tensor_scalar(result[:, cols], window[:, cols], gain[:], shift[:], MULT, ADD)
+            queue.dma_start(out[:, cols], result[:, cols])

@@ -14,6 +14,7 @@ KB = K // P
 HB = KB // 2
 WARM = 8
 QC = Q // 16
+ROW_ALIGN = 256
 
 FLOPS = 2 * K * P * N
 
@@ -36,18 +37,18 @@ def tile_scatter_matmul_kernel(tc, base, x, w, s, b, offs, out):
         ident = held.tile([P, P], BF16, name="ident")
         make_identity(nc, ident[:])
 
-        base_sb = held.tile([P, S], BF16, name="base_sb")
+        base_sb = held.tile([P, S], BF16, name="base_sb", align_bytes=ROW_ALIGN)
         nc.scalar.dma_start(base_sb[:], base)
 
         x_view = x.rearrange("(p kb) n -> p kb n", kb=KB)
         x_sb, w_sb = [], []
         for h in range(2):
             blocks = slice(h * HB, (h + 1) * HB)
-            x_h = held.tile([P, HB, N], BF16, name=f"x{h}")
+            x_h = held.tile([P, HB, N], BF16, name=f"x{h}", align_bytes=ROW_ALIGN)
             (nc.sync if h == 0 else nc.scalar).dma_start(x_h[:], x_view[:, blocks, :])
             x_sb.append(x_h)
             for e in range(E):
-                w_he = held.tile([P, HB, P], BF16, name=f"w{h}_{e}")
+                w_he = held.tile([P, HB, P], BF16, name=f"w{h}_{e}", align_bytes=ROW_ALIGN)
                 queue = nc.scalar if e % 2 == 0 else nc.sync
                 queue.dma_start(w_he[:], w[e].rearrange("(p kb) m -> p kb m", kb=KB)[:, blocks, :])
                 w_sb.append(w_he)
@@ -72,7 +73,7 @@ def tile_scatter_matmul_kernel(tc, base, x, w, s, b, offs, out):
                         stop=(h == 1 and e == E - 1 and q == HB - 1),
                     )
 
-        result = held.tile([P, S], F32, name="result")
+        result = held.tile([P, S], F32, name="result", align_bytes=ROW_ALIGN)
         for half, queue in enumerate((nc.sync, nc.scalar)):
             cols = slice(half * (S // 2), (half + 1) * (S // 2))
             nc.vector.tensor_scalar(result[:, cols], window[:, cols], gain[:], shift[:], MULT, ADD)

@@ -41,17 +41,21 @@ def tile_scatter_matmul_kernel(tc, base, x, w, s, b, offs, out):
         nc.scalar.dma_start(base_sb[:], base)
 
         x_view = x.rearrange("(p kb) n -> p kb n", kb=KB)
-        x_sb, w_sb = [], []
+        x_sb, w_sb = [], {}
+        last = held.tile([P, KB, P], BF16, name="w_last", align_bytes=ROW_ALIGN)
         for h in range(2):
             blocks = slice(h * HB, (h + 1) * HB)
             x_h = held.tile([P, HB, N], BF16, name=f"x{h}", align_bytes=ROW_ALIGN)
             (nc.sync if h == 0 else nc.scalar).dma_start(x_h[:], x_view[:, blocks, :])
             x_sb.append(x_h)
-            for e in range(E):
+            for e in range(E - 1):
                 w_he = held.tile([P, HB, P], BF16, name=f"w{h}_{e}", align_bytes=ROW_ALIGN)
                 queue = nc.scalar if e % 2 == 0 else nc.sync
                 queue.dma_start(w_he[:], w[e].rearrange("(p kb) m -> p kb m", kb=KB)[:, blocks, :])
-                w_sb.append(w_he)
+                w_sb[h, e] = w_he[:]
+            if h == 0:
+                nc.sync.dma_start(last[:], w[E - 1].rearrange("(p kb) m -> p kb m", kb=KB))
+            w_sb[h, E - 1] = last[:, blocks, :]
 
         gain = held.tile([P, 1], F32, name="gain")
         nc.scalar.dma_start(gain[:], s)
@@ -61,17 +65,16 @@ def tile_scatter_matmul_kernel(tc, base, x, w, s, b, offs, out):
         window = psum.tile([P, S], F32, name="window")
         nc.tensor.matmul(window[:], ident[:], base_sb[:], start=True, stop=False)
 
-        for h in range(2):
-            for e in range(E):
-                piece = offsets[:, e * QC : (e + 1) * QC]
-                for q in range(HB):
-                    nc.tensor.matmul(
-                        window[:].indirect(piece),
-                        w_sb[h * E + e][:, q, :],
-                        x_sb[h][:, q, e * Q : (e + 1) * Q],
-                        start=False,
-                        stop=(h == 1 and e == E - 1 and q == HB - 1),
-                    )
+        passes = [(0, e) for e in range(E)] + [(1, E - 1)] + [(1, e) for e in range(E - 1)]
+        for turn, (h, e) in enumerate(passes):
+            for q in range(HB):
+                nc.tensor.matmul(
+                    window[:].indirect(offsets[:, e * QC : (e + 1) * QC]),
+                    w_sb[h, e][:, q, :],
+                    x_sb[h][:, q, e * Q : (e + 1) * Q],
+                    start=False,
+                    stop=(turn == len(passes) - 1 and q == HB - 1),
+                )
 
         result = held.tile([P, S], F32, name="result", align_bytes=ROW_ALIGN)
         for half, queue in enumerate((nc.sync, nc.scalar)):

@@ -77,7 +77,8 @@ def tile_scatter_matmul_kernel(tc, base, x, w, s, b, offs, out):
                 )
 
         result = held.tile([P, S], F32, name="result", align_bytes=ROW_ALIGN)
-        for half, queue in enumerate((nc.sync, nc.scalar)):
-            cols = slice(half * (S // 2), (half + 1) * (S // 2))
+        parts = [(0, S // 2, nc.sync), (S // 2, S // 4, nc.scalar), (3 * S // 4, S // 4, nc.sync)]
+        for first, width, queue in parts:
+            cols = slice(first, first + width)
             nc.vector.tensor_scalar(result[:, cols], window[:, cols], gain[:], shift[:], MULT, ADD)
             queue.dma_start(out[:, cols], result[:, cols])

@@ -46,7 +46,7 @@ def tile_scatter_matmul_kernel(tc, base, x, w, s, b, offs, out):
         for h in range(2):
             blocks = slice(h * HB, (h + 1) * HB)
             x_h = held.tile([P, HB, N], BF16, name=f"x{h}", align_bytes=ROW_ALIGN)
-            (nc.sync if h == 0 else nc.scalar).dma_start(x_h[:], x_view[:, blocks, :])
+            nc.sync.dma_start(x_h[:], x_view[:, blocks, :])
             x_sb.append(x_h)
             for e in range(E - 1):
                 w_he = held.tile([P, HB, P], BF16, name=f"w{h}_{e}", align_bytes=ROW_ALIGN)
@@ -54,7 +54,7 @@ def tile_scatter_matmul_kernel(tc, base, x, w, s, b, offs, out):
                 queue.dma_start(w_he[:], w[e].rearrange("(p kb) m -> p kb m", kb=KB)[:, blocks, :])
                 w_sb[h, e] = w_he[:]
             if h == 0:
-                nc.sync.dma_start(last[:], w[E - 1].rearrange("(p kb) m -> p kb m", kb=KB))
+                nc.scalar.dma_start(last[:], w[E - 1].rearrange("(p kb) m -> p kb m", kb=KB))
             w_sb[h, E - 1] = last[:, blocks, :]
 
         gain = held.tile([P, 1], F32, name="gain")

import concourse.mybir as mybir
from concourse.masks import make_identity

BF16, F32, U16 = mybir.dt.bfloat16, mybir.dt.float32, mybir.dt.uint16
MULT, ADD = mybir.AluOpType.mult, mybir.AluOpType.add

P = 128
S = 512
K = 512
N = 384
E = 4
Q = N // E
KB = K // P
HB = KB // 2
WARM = 8
QC = Q // 16
ROW_ALIGN = 256

FLOPS = 2 * K * P * N


def tile_scatter_matmul_kernel(tc, base, x, w, s, b, offs, out):
    nc = tc.nc
    with (
        tc.tile_pool(name="held", bufs=1) as held,
        tc.psum_pool(name="psum", bufs=1) as psum,
    ):
        offsets = held.tile([P, N // 16], U16, name="offsets")
        nc.sync.dma_start(offsets[:], offs)

        zeros = held.tile([P, P], BF16, name="zeros")
        nc.vector.memset(zeros[:], 0.0)
        spare = psum.tile([P, P], F32, name="spare")
        for i in range(WARM):
            nc.tensor.matmul(spare[:], zeros[:], zeros[:], start=True, stop=True)

        ident = held.tile([P, P], BF16, name="ident")
        make_identity(nc, ident[:])

        base_sb = held.tile([P, S], BF16, name="base_sb", align_bytes=ROW_ALIGN)
        nc.scalar.dma_start(base_sb[:], base)

        x_view = x.rearrange("(p kb) n -> p kb n", kb=KB)
        x_sb, w_sb = [], {}
        last = held.tile([P, KB, P], BF16, name="w_last", align_bytes=ROW_ALIGN)
        for h in range(2):
            blocks = slice(h * HB, (h + 1) * HB)
            x_h = held.tile([P, HB, N], BF16, name=f"x{h}", align_bytes=ROW_ALIGN)
            nc.sync.dma_start(x_h[:], x_view[:, blocks, :])
            x_sb.append(x_h)
            for e in range(E - 1):
                w_he = held.tile([P, HB, P], BF16, name=f"w{h}_{e}", align_bytes=ROW_ALIGN)
                queue = nc.scalar if e % 2 == 0 else nc.sync
                queue.dma_start(w_he[:], w[e].rearrange("(p kb) m -> p kb m", kb=KB)[:, blocks, :])
                w_sb[h, e] = w_he[:]
            if h == 0:
                nc.scalar.dma_start(last[:], w[E - 1].rearrange("(p kb) m -> p kb m", kb=KB))
            w_sb[h, E - 1] = last[:, blocks, :]

        gain = held.tile([P, 1], F32, name="gain")
        nc.scalar.dma_start(gain[:], s)
        shift = held.tile([P, 1], F32, name="shift")
        nc.sync.dma_start(shift[:], b)

        window = psum.tile([P, S], F32, name="window")
        nc.tensor.matmul(window[:], ident[:], base_sb[:], start=True, stop=False)

        passes = [(0, e) for e in range(E)] + [(1, E - 1)] + [(1, e) for e in range(E - 1)]
        for turn, (h, e) in enumerate(passes):
            for q in range(HB):
                nc.tensor.matmul(
                    window[:].indirect(offsets[:, e * QC : (e + 1) * QC]),
                    w_sb[h, e][:, q, :],
                    x_sb[h][:, q, e * Q : (e + 1) * Q],
                    start=False,
                    stop=(turn == len(passes) - 1 and q == HB - 1),
                )

        result = held.tile([P, S], F32, name="result", align_bytes=ROW_ALIGN)
        parts = [(0, S // 2, nc.sync), (S // 2, S // 4, nc.scalar), (3 * S // 4, S // 4, nc.sync)]
        for first, width, queue in parts:
            cols = slice(first, first + width)
            nc.vector.tensor_scalar(result[:, cols], window[:, cols], gain[:], shift[:], MULT, ADD)
            queue.dma_start(out[:, cols], result[:, cols])
